import numpy as np
import ml_dtypes


def mxq(x, axis, fmt="e4m3"):
    dtype, down = {"e4m3": (ml_dtypes.float8_e4m3fn, 7), "e5m2": (ml_dtypes.float8_e5m2, 14)}[fmt]
    v = np.moveaxis(np.asarray(x, np.float32).astype(ml_dtypes.bfloat16).astype(np.float64), axis, -1)
    blocks = v.reshape(v.shape[:-1] + (-1, 32))
    amax = np.abs(blocks).max(-1, keepdims=True)
    byte = np.maximum(np.where(amax > 0, np.frexp(amax)[1] - 1 + 127, 0) - down, 1)
    scale = np.exp2(byte - 127.0)
    codes = (blocks / scale).astype(np.float32).astype(dtype).astype(np.float64)
    return np.moveaxis((codes * scale).reshape(v.shape), -1, axis)


WIDE = False


def mx_kscale(k):
    if not WIDE:
        return np.ones(k)
    levels = np.array([10, -10, 5, -5, 0])
    if k % 512:
        return np.exp2(np.random.permutation(np.resize(levels, k // 32))).repeat(32)
    a = np.empty((k // 512, 16))
    for p in range(k // 512):
        a[p, :8] = np.random.permutation(np.resize(levels, 8))
        for g in range(8):
            far = levels[np.abs(levels - a[p, g]) >= 10]
            a[p, g + 8] = far[np.random.randint(len(far))]
    return np.exp2(a.ravel()).repeat(32)


def f64(x):
    return np.asarray(x).astype(np.float64)


def striped(idx):
    return np.tile(idx.reshape(-1, 16).T, (8, 1)).astype(np.uint16)


def unstriped(offs):
    return offs[:16].T.reshape(-1).astype(np.int64)


def relu2(v):
    return np.maximum(v, 0.0) ** 2


K, T, E, C, H, N = 512, 1536, 8, 128, 512, 512


def by_expert(wq, xq):
    return np.concatenate([wq[e].T @ xq[:, e * C:(e + 1) * C] for e in range(E)], axis=1)


def setup_inputs():
    n = np.random.standard_normal
    s = mx_kscale(K)[:, None]
    u = mx_kscale(H)
    return {
        "xT": (n((K, T)) * s).astype(np.float32),
        "w1": (n((E + 1, K, H)) / np.sqrt(K) / s[None] * u[None, None, :]).astype(np.float32),
        "w2": (n((E + 1, H, N)) / np.sqrt(H) / u[None, :, None] ** 2).astype(np.float32),
        "gate": np.tile(np.random.uniform(0.2, 1.0, E * C), (N, 1)).astype(np.float32),
        "offs": striped(np.random.permutation(T)[:E * C]),
    }


def reference(xT, w1, w2, gate, offs):
    idx = unstriped(offs)
    w1q, w2q = mxq(f64(w1), 1, "e4m3"), mxq(f64(w2), 1, "e4m3")
    xs = mxq(f64(xT), 0, "e4m3")
    hs = relu2(w1q[E].T @ xs)
    ys = w2q[E].T @ mxq(hs, 0, "e4m3")
    xq = mxq(f64(xT)[:, idx], 0, "e4m3")
    h = relu2(by_expert(w1q, xq))
    y = by_expert(w2q, mxq(h, 0, "e4m3"))
    out = ys
    out[:, idx] += f64(gate) * y
    return out

from contextlib import ExitStack

import concourse.mybir as mybir

K, T, E, C, H, N = 512, 1536, 8, 128, 512, 512
S = E * C
FLOPS = 2 * (S + T) * (K * H + H * N)
BYTES = 4 * (K * T + (E + 1) * (K * H + H * N) + S + N * T) + 2 * 128 * (S // 16)

F32 = mybir.dt.float32
BF16 = mybir.dt.bfloat16
U32 = mybir.dt.uint32
U16 = mybir.dt.uint16
U8 = mybir.dt.uint8
FP8X4 = mybir.dt.float8_e4m3fn_x4
ADD, MULT = mybir.AluOpType.add, mybir.AluOpType.mult
RELU = mybir.ActivationFunctionType.Relu
SQUARE = mybir.ActivationFunctionType.Square

P = 128
PACK = 4
HALF = 512
PIECE = 256
CHUNK = 512


def tile_moe_shr_mlp_relu2_kernel(tc, xT, w1, w2, gate, offs, out):
    nc = tc.nc
    with ExitStack() as ctx:
        held = ctx.enter_context(tc.tile_pool(name="held", bufs=1))
        rawp = ctx.enter_context(tc.tile_pool(name="rawp", bufs=7))
        wbp = ctx.enter_context(tc.tile_pool(name="wbp", bufs=4))
        wcp = ctx.enter_context(tc.tile_pool(name="wcp", bufs=6))
        two = ctx.enter_context(tc.tile_pool(name="two", bufs=2))
        three = ctx.enter_context(tc.tile_pool(name="three", bufs=3))
        outp = ctx.enter_context(tc.tile_pool(name="outp", bufs=4))
        ps_a = ctx.enter_context(tc.psum_pool(name="ps_a", bufs=2))
        ps_y = ctx.enter_context(tc.psum_pool(name="ps_y", bufs=2))
        ps_s = ctx.enter_context(tc.psum_pool(name="ps_s", bufs=4))

        offsets = held.tile([P, S // 16], U16, name="offsets")
        nc.sync.dma_start(offsets[:], offs)

        x_raw = held.tile([P, PACK, T], F32, name="x_raw")
        x_rows = xT.rearrange("(p j) t -> p j t", j=PACK)
        for j in range(PACK):
            nc.sync.dma_start(out=x_raw[:, j, :], in_=x_rows[:, j, :])

        z = [held.tile([P, T], F32, name=f"z{b}") for b in range(N // P)]
        for b in range(N // P):
            nc.vector.memset(z[b][:], 0.0)

        gate_sb = held.tile([P, S], F32, name="gate_sb")
        slot_codes = held.tile([P, S], U32, name="slot_codes", align_bytes=64)
        slot_scales = held.tile([P, S], U8, name="slot_scales", align_bytes=64)
        tok_codes = held.tile([P, T], U32, name="tok_codes", align_bytes=64)
        tok_scales = held.tile([P, T], U8, name="tok_scales", align_bytes=64)
        hs_codes = held.tile([P, T], U32, name="hs_codes", align_bytes=64)
        hs_scales = held.tile([P, T], U8, name="hs_scales", align_bytes=64)

        def copy_on(engine, dst, src):
            if engine == "S":
                nc.scalar.copy(out=dst, in_=src)
            elif engine == "G":
                nc.gpsimd.tensor_scalar(out=dst, in0=src, scalar1=1.0, scalar2=0.0, op0=MULT, op1=ADD)
            else:
                nc.vector.tensor_copy(out=dst, in_=src)

        def load(w, e):
            raw = rawp.tile([P, PACK, 512], F32, name="raw")
            nc.sync.dma_start(out=raw[:], in_=w[e].rearrange("(p j) c -> p j c", j=PACK))
            return raw

        def interleave(raw, permute, shares):
            wb = wbp.tile([P, PACK * 512], BF16, name="wb", align_bytes=64)
            if permute:
                dst = wb[:].rearrange("p (t m j) -> p m j t", t=PACK, j=PACK)
                src = raw[:].rearrange("p j (m t) -> p m j t", t=PACK)
            else:
                dst = wb[:].rearrange("p (m i j) -> p m j i", i=4, j=PACK)
                src = raw[:].rearrange("p j (m i) -> p m j i", i=4)
            for engine, a, b in shares:
                copy_on(engine, dst[:, a:b], src[:, a:b])
            return wb

        def quantize(wb, pool=wcp, name="wc"):
            codes = pool.tile([P, 512], U32, name=name, align_bytes=64)
            scales = pool.tile([P, 512], U8, name=name + "_s", align_bytes=64)
            nc.vector.quantize_mx(out=codes[:].bitcast(FP8X4), scales=scales[:], in_=wb[:])
            return codes, scales

        def mx(dst, w, cols, x_codes, x_scales, xcols):
            nc.tensor.matmul_mx(
                out=dst,
                lhsT=w[0][:, cols].bitcast(FP8X4),
                lhsT_scale=w[1][:, cols],
                rhs=x_codes[:, xcols].bitcast(FP8X4),
                rhs_scale=x_scales[:, xcols],
                start=True,
                stop=True,
            )

        W1_SHARES = [("S", 0, 96), ("G", 96, 128)]
        W2_SHARES = [("G", 0, 32), ("G", 32, 64), ("G", 64, 96), ("G", 96, 128)]

        g4 = []
        for h in range(2):
            g4_tile = two.tile([P, PACK, HALF], F32, name="g4")
            g4.append(g4_tile)
        for j in range(PACK):
            for h in range(2):
                o = offsets[:, h * (HALF // 16) : (h + 1) * (HALF // 16)]
                nc.vector.tensor_copy(g4[h][:, j, :], x_raw[:, j, :].indirect(o))

        order = [("1", 0), ("2", 0), ("g", 0), ("1", 1), ("2", 1), ("1", E), ("1", 2), ("2", 2), ("1", 3), ("2", 3),
                 ("2", E), ("1", 4), ("2", 4), ("1", 5), ("2", 5), ("1", 6), ("2", 6), ("1", 7), ("2", 7)]
        raws = {}
        bfs = {}
        pos = [0]

        def advance(n):
            for _ in range(n):
                if pos[0] < len(order):
                    kind, e = order[pos[0]]
                    pos[0] += 1
                    if kind == "g":
                        nc.sync.dma_start(out=gate_sb[:], in_=gate[0:P, :])
                        kind, e = order[pos[0]]
                        pos[0] += 1
                    raws[kind, e] = load(w1 if kind == "1" else w2, e)

        def prepare(kind, e):
            bfs[kind, e] = interleave(raws[kind, e], kind == "1", W1_SHARES if kind == "1" else W2_SHARES)

        advance(6)

        for h in range(2):
            xb = two.tile([P, PACK * HALF], BF16, name="xb", align_bytes=64)
            dst = xb[:].rearrange("p (m i j) -> p m j i", i=4, j=PACK)
            src = g4[h][:].rearrange("p j (m i) -> p m j i", i=4)
            copy_on("S", dst[:, 0:64], src[:, 0:64])
            copy_on("G", dst[:, 64:96], src[:, 64:96])
            copy_on("G", dst[:, 96:128], src[:, 96:128])
            cols = slice(h * HALF, (h + 1) * HALF)
            nc.vector.quantize_mx(out=slot_codes[:, cols].bitcast(FP8X4), scales=slot_scales[:, cols], in_=xb[:])

        prepare("1", 0)
        prepare("2", 0)

        shared = {}

        def shared_piece(i):
            t0 = i * PIECE
            cols = slice(t0, t0 + PIECE)
            tb = two.tile([P, PACK * PIECE], BF16, name="tb", align_bytes=64)
            dst = tb[:].rearrange("p (m i j) -> p m j i", i=4, j=PACK)
            src = x_raw[:, :, cols].rearrange("p j (m i) -> p m j i", i=4)
            copy_on("G", dst[:, 0:32], src[:, 0:32])
            copy_on("G", dst[:, 32:64], src[:, 32:64])
            nc.vector.quantize_mx(out=tok_codes[:, cols].bitcast(FP8X4), scales=tok_scales[:, cols], in_=tb[:])
            rs = two.tile([P, PACK, PIECE], F32, name="rs")
            for a in range(2):
                bank = ps_s.tile([P, 2, PIECE], F32, name="bank_s")
                for u in range(2):
                    t = 2 * a + u
                    mx(bank[:, u, :], shared["1"], slice(t * P, (t + 1) * P), tok_codes, tok_scales, cols)
                nc.scalar.activation(rs[:, 2 * a : 2 * a + 2, :], bank[:], RELU)
            hsb = two.tile([P, PACK * PIECE], BF16, name="hsb", align_bytes=64)
            nc.scalar.activation(
                hsb[:].rearrange("p (m i t) -> p m t i", i=4, t=PACK),
                rs[:].rearrange("p t (m i) -> p m t i", i=4),
                SQUARE,
            )
            nc.vector.quantize_mx(out=hs_codes[:, cols].bitcast(FP8X4), scales=hs_scales[:, cols], in_=hsb[:])

        pending = []
        done = [0]

        def scatter(n):
            for _ in range(n):
                if done[0] < len(pending):
                    pair, b, values = pending[done[0]]
                    done[0] += 1
                    o = offsets[:, pair * 16 : (pair + 1) * 16]
                    nc.vector.tensor_copy(z[b][:].indirect(o), values[:, b, :])

        yg = None
        for e in range(E):
            w1q = quantize(bfs["1", e])
            slots = slice(e * C, (e + 1) * C)
            bank_a = ps_a.tile([P, PACK, C], F32, name="bank_a")
            for t in range(PACK):
                mx(bank_a[:, t, :], w1q, slice(t * P, (t + 1) * P), slot_codes, slot_scales, slots)
            r = three.tile([P, PACK, C], F32, name="r")
            nc.scalar.activation(r[:], bank_a[:], RELU)
            hb = three.tile([P, PACK * C], BF16, name="hb", align_bytes=64)
            nc.scalar.activation(
                hb[:].rearrange("p (m i t) -> p m t i", i=4, t=PACK),
                r[:].rearrange("p t (m i) -> p m t i", i=4),
                SQUARE,
            )
            scatter(1)
            advance(2)
            if e == 1:
                advance(1)
                bfs["1", E] = interleave(raws["1", E], True, W1_SHARES)
                shared["1"] = quantize(bfs["1", E], held, "ws1")
            if e == 4:
                advance(1)
                bfs["2", E] = interleave(raws["2", E], False, W2_SHARES)
                shared["2"] = quantize(bfs["2", E], held, "ws2")
            if e + 1 < E:
                prepare("1", e + 1)
                prepare("2", e + 1)
            w2q = quantize(bfs["2", e])
            hc = three.tile([P, C], U32, name="hc", align_bytes=64)
            hc_s = three.tile([P, C], U8, name="hc_s", align_bytes=64)
            nc.vector.quantize_mx(out=hc[:].bitcast(FP8X4), scales=hc_s[:], in_=hb[:])
            bank_y = ps_y.tile([P, N // P, C], F32, name="bank_y")
            for b in range(N // P):
                mx(bank_y[:, b, :], w2q, slice(b * P, (b + 1) * P), hc, hc_s, slice(0, C))
            scatter(1)
            if e % 2 == 0:
                yg = two.tile([P, N // P, 2 * C], F32, name="yg")
            half = slice((e % 2) * C, (e % 2 + 1) * C)
            nc.vector.tensor_tensor(
                out=yg[:, :, half],
                in0=bank_y[:],
                in1=gate_sb[:, slots].unsqueeze(1).to_broadcast([P, N // P, C]),
                op=MULT,
            )
            if e % 2 == 1:
                for b in range(N // P):
                    pending.append((e // 2, b, yg))
            if e >= 2:
                shared_piece(e - 2)

        for b in range(N // P):
            scatter(1)
            for c in range(T // CHUNK):
                cols = slice(c * CHUNK, (c + 1) * CHUNK)
                bank = ps_s.tile([P, CHUNK], F32, name="bank_s")
                mx(bank[:], shared["2"], slice(b * P, (b + 1) * P), hs_codes, hs_scales, cols)
                o_sb = outp.tile([P, CHUNK], F32, name="o_sb")
                nc.vector.tensor_tensor(out=o_sb[:], in0=bank[:], in1=z[b][:, cols], op=ADD)
                nc.sync.dma_start(out=out[b * P : (b + 1) * P, cols], in_=o_sb[:])
